import numpy as np
import ml_dtypes


def mxq(x, axis, fmt="e4m3"):
    dtype, down = {"e4m3": (ml_dtypes.float8_e4m3fn, 7), "e5m2": (ml_dtypes.float8_e5m2, 14)}[fmt]
    v = np.moveaxis(np.asarray(x, np.float32).astype(ml_dtypes.bfloat16).astype(np.float64), axis, -1)
    blocks = v.reshape(v.shape[:-1] + (-1, 32))
    amax = np.abs(blocks).max(-1, keepdims=True)
    byte = np.maximum(np.where(amax > 0, np.frexp(amax)[1] - 1 + 127, 0) - down, 1)
    scale = np.exp2(byte - 127.0)
    codes = (blocks / scale).astype(np.float32).astype(dtype).astype(np.float64)
    return np.moveaxis((codes * scale).reshape(v.shape), -1, axis)


WIDE = False


def mx_kscale(k):
    if not WIDE:
        return np.ones(k)
    levels = np.array([10, -10, 5, -5, 0])
    if k % 512:
        return np.exp2(np.random.permutation(np.resize(levels, k // 32))).repeat(32)
    a = np.empty((k // 512, 16))
    for p in range(k // 512):
        a[p, :8] = np.random.permutation(np.resize(levels, 8))
        for g in range(8):
            far = levels[np.abs(levels - a[p, g]) >= 10]
            a[p, g + 8] = far[np.random.randint(len(far))]
    return np.exp2(a.ravel()).repeat(32)


def f64(x):
    return np.asarray(x).astype(np.float64)


def striped(idx):
    return np.tile(idx.reshape(-1, 16).T, (8, 1)).astype(np.uint16)


def unstriped(offs):
    return offs[:16].T.reshape(-1).astype(np.int64)


def striped8(idx):
    return np.concatenate([x.reshape(-1, 16).T for x in idx]).astype(np.uint16)


def runs(offs, k):
    lists = np.stack([offs[16 * r : 16 * r + 16].T.reshape(-1) for r in range(8)]).astype(np.int64)
    return lists[np.arange(k) % 512 // 64]


def pack_weight(w):
    k, n = w.shape
    w = f64(np.asarray(w, np.float32).astype(ml_dtypes.bfloat16)).reshape(k // 32, 32, n)
    amax = np.abs(w).max(1)
    byte = np.clip(np.where(amax > 0, np.frexp(amax)[1] - 1 + 127 - 7, 1), 1, 254)
    scaled = (w * np.exp2(127.0 - byte)[:, None, :]).reshape(k, n).astype(np.float32)
    words = np.ascontiguousarray(scaled.reshape(k // 512, 128, 4, n).transpose(0, 1, 3, 2)).astype(ml_dtypes.float8_e4m3fn).view(np.uint8)
    return words, np.ascontiguousarray(byte.astype(np.uint8).reshape(k // 512, 16, n))


def unpack_weight(words, scales):
    g, p, n, _ = words.shape
    vals = np.ascontiguousarray(words).view(ml_dtypes.float8_e4m3fn).astype(np.float64) * np.repeat(np.exp2(scales.astype(np.float64) - 127.0), 8, axis=1)[..., None]
    return vals.transpose(0, 1, 3, 2).reshape(g * 512, n)

def planes(y):
    n, m = y.shape
    v = y.astype(np.float32).astype(ml_dtypes.bfloat16).astype(np.float64).reshape(n // 32, 32, m)
    top = np.abs(v).max(1)
    byte = np.clip(np.where(top > 0, np.frexp(top)[1] - 1 + 127 - 7, 1), 1, 254)
    codes = (v * np.exp2(127.0 - byte)[:, None, :]).reshape(n, m).astype(np.float32).astype(ml_dtypes.float8_e4m3fn).view(np.uint8)
    words = codes.reshape(n // 512, 128, 4, m).transpose(0, 1, 3, 2)
    return np.ascontiguousarray(words), np.ascontiguousarray(byte.astype(np.uint8).reshape(n // 512, 16, m))


K, T, S, N, W = 512, 2048, 256, 512, 128


def setup_inputs():
    n = np.random.standard_normal
    s = mx_kscale(K)[:, None]
    packed_xT = pack_weight(n((K, T)) * s)
    perm = np.random.permutation(S)
    return {
        "x_words": packed_xT[0],
        "x_scales": packed_xT[1],
        "w1": (n((K, N)) / np.sqrt(2 * K) / s).astype(np.float32),
        "w2": (n((K, N)) / np.sqrt(2 * K) / s).astype(np.float32),
        "offs": striped(np.random.permutation(T)[:S]),
        "hz": striped8(np.random.randint(0, T, (8, S))),
        "n1": striped(perm[:W]),
        "n2": striped(perm[W:]),
    }


def reference(x_words, x_scales, w1, w2, offs, hz, n1, n2):
    xq = unpack_weight(x_words, x_scales)[:, unstriped(offs)]
    x_hz = unpack_weight(x_words, x_scales)[np.arange(K)[:, None], runs(hz, K)]
    h = mxq(f64(w1), 0, "e4m3").T @ xq + mxq(f64(w2), 0, "e4m3").T @ x_hz
    pa = h[:, unstriped(n1)]
    pb = h[:, unstriped(n2)]
    rb = pa - pb
    ra = 0.75 * (pa + pb)
    ds = np.zeros((N, S))
    ds[:, unstriped(n1)] = ra
    out = ds.copy()
    out[:, unstriped(n2)] = rb
    return (out,) + planes(out)

@@ -1,0 +1,158 @@
+from contextlib import ExitStack
+
+import concourse.mybir as mybir
+
+K, T, S, N, W = 512, 2048, 256, 512, 128
+FLOPS = 2 * 2 * K * N * S
+
+F32 = mybir.dt.float32
+BF16 = mybir.dt.bfloat16
+I32 = mybir.dt.int32
+U32 = mybir.dt.uint32
+U16 = mybir.dt.uint16
+U8 = mybir.dt.uint8
+FP8X4 = mybir.dt.float8_e4m3fn_x4
+COPY = mybir.ActivationFunctionType.Copy
+ADD = mybir.AluOpType.add
+SUB = mybir.AluOpType.subtract
+
+P = 128
+PACK = 4
+HALF = N // 2
+HP = P // 2
+
+
+def tile_picked_othhaar_none_po_kernel(tc, x_words, x_scales, w1, w2, offs, hz, n1, n2, out_0, out_1, out_2):
+    nc = tc.nc
+    with ExitStack() as ctx:
+        keep = ctx.enter_context(tc.tile_pool(name="keep", bufs=1))
+        psum = ctx.enter_context(tc.psum_pool(name="psum", bufs=1))
+
+        def sb(name, shape, dtype):
+            return keep.tile(shape, dtype, name=name, align_bytes=64)
+
+        hz_t = sb("hz_t", [P, S // 16], U16)
+        offs_t = sb("offs_t", [P, S // 16], U16)
+        n1_t = sb("n1_t", [P, W // 16], U16)
+        n2_t = sb("n2_t", [P, W // 16], U16)
+        nc.sync.dma_start(hz_t[:], hz)
+        nc.sync.dma_start(offs_t[:], offs)
+
+        raw = {(i, u): sb("raw%d%d" % (i, u), [P, PACK, HALF], F32) for i in range(2) for u in range(2)}
+
+        def load_weight_half(i, u):
+            rows = (w1, w2)[i].rearrange("(p j) c -> p j c", j=PACK)
+            nc.sync.dma_start(raw[i, u][:], rows[:, :, u * HALF:(u + 1) * HALF])
+
+        table_scales = sb("table_scales", [P, T], U8)
+        nc.vector.memset(table_scales[:].bitcast(I32), 0)
+        load_weight_half(0, 0)
+        rows_by_run = x_scales[0].rearrange("(r e) c -> e r c", e=2)
+        for e in range(2):
+            nc.sync.dma_start(table_scales[e:P:16, :].bitcast(I32), rows_by_run[e].bitcast(I32))
+
+        table_words = sb("table_words", [P, T], U32)
+        nc.sync.dma_start(table_words[:].bitcast(I32), x_words[0].rearrange("p c r -> p (c r)").bitcast(I32))
+        load_weight_half(1, 0)
+        load_weight_half(0, 1)
+        load_weight_half(1, 1)
+        nc.sync.dma_start(n1_t[:], n1)
+        nc.sync.dma_start(n2_t[:], n2)
+
+        picked_scales = sb("picked_scales", [P, 2 * S], U8)
+        nc.vector.tensor_copy(picked_scales[:, S:2 * S], table_scales[:].indirect(hz_t[:]))
+        nc.vector.tensor_copy(picked_scales[:, 0:S], table_scales[:].indirect(offs_t[:]))
+        x_sc = sb("x_sc", [P, 2 * S], U8)
+        nc.vector.tensor_copy(x_sc[:].bitcast(I32), picked_scales[:].bitcast(I32))
+        for e in range(2):
+            nc.scalar.dma_start(x_sc[2 + e:P:32, :].bitcast(I32), picked_scales[16 + e:P:32, :].bitcast(I32))
+
+        x_w = [sb("x_w%d" % i, [P, S], U32) for i in range(2)]
+        nc.vector.tensor_copy(x_w[0][:], table_words[:].indirect(offs_t[:]))
+        nc.vector.tensor_copy(x_w[1][:], table_words[:].indirect(hz_t[:]))
+
+        low_bf = {(i, u): sb("low_bf%d%d" % (i, u), [P, P * PACK], BF16) for i in range(2) for u in range(2)}
+        low_c = {(i, u): sb("low_c%d%d" % (i, u), [P, P], U32) for i in range(2) for u in range(2)}
+        low_s = {(i, u): sb("low_s%d%d" % (i, u), [P, P], U8) for i in range(2) for u in range(2)}
+        high_bf = [sb("high_bf%d" % i, [P, 2 * P * PACK], BF16) for i in range(2)]
+        high_c = [sb("high_c%d" % i, [P, 2 * P], U32) for i in range(2)]
+        high_s = [sb("high_s%d" % i, [P, 2 * P], U8) for i in range(2)]
+
+        def cast(on_scalar, out, in_):
+            if on_scalar:
+                nc.scalar.copy(out, in_)
+            else:
+                nc.vector.tensor_copy(out, in_)
+
+        def cast_low(i, u, on_scalar):
+            src = raw[i, u][:].rearrange("p j (m s) -> p m j s", s=PACK)[:, :, :, 0:2]
+            cast(on_scalar, low_bf[i, u][:].rearrange("p (m s j) -> p m j s", s=2, j=PACK), src)
+
+        def cast_high(i, u, on_scalar):
+            src = raw[i, u][:].rearrange("p j (m s) -> p m j s", s=PACK)[:, :, :, 2:4]
+            dst = high_bf[i][:].rearrange("p (s m j) -> p m j s", s=2, j=PACK)[:, u * HP:(u + 1) * HP, :, :]
+            cast(on_scalar, dst, src)
+
+        def quantize(codes, scales, values):
+            nc.vector.quantize_mx(out=codes[:].bitcast(FP8X4), scales=scales[:], in_=values[:])
+
+        def project(name, codes, scales):
+            acc = psum.tile([P, S], F32, name="acc" + name)
+            for i in range(2):
+                nc.tensor.matmul_mx(out=acc[:], lhsT=codes[i].bitcast(FP8X4), lhsT_scale=scales[i],
+                                    rhs=x_w[i][:].bitcast(FP8X4), rhs_scale=x_sc[:, i * S:(i + 1) * S],
+                                    start=(i == 0), stop=(i == 1))
+            h = sb("h" + name, [P, S], F32)
+            nc.vector.tensor_copy(h[:], acc[:])
+            return h
+
+        def haar(name, h):
+            pa = sb("pa" + name, [P, W], F32)
+            pb = sb("pb" + name, [P, W], F32)
+            nc.scalar.activation(pa[:], h[:].indirect(n1_t[:]), COPY)
+            nc.scalar.activation(pb[:], h[:].indirect(n2_t[:]), COPY)
+            total = sb("total" + name, [P, W], F32)
+            rb = sb("rb" + name, [P, W], F32)
+            nc.vector.tensor_tensor(total[:], pa[:], pb[:], ADD)
+            nc.vector.tensor_tensor(rb[:], pa[:], pb[:], SUB)
+            y = sb("y" + name, [P, S], F32)
+            nc.scalar.activation(y[:].indirect(n1_t[:]), total[:], COPY, scale=0.75)
+            nc.scalar.activation(y[:].indirect(n2_t[:]), rb[:], COPY)
+            return y
+
+        out_rows = out_0.rearrange("(p s) c -> p s c", s=PACK)
+        y_low = sb("y_low", [P, 2, S], F32)
+        y_bf = sb("y_bf", [P, S, PACK], BF16)
+
+        for u in range(2):
+            cast_low(0, u, u == 0)
+            quantize(low_c[0, u], low_s[0, u], low_bf[0, u])
+            if u == 0:
+                cast_high(0, u, True)
+            cast_low(1, u, False)
+            quantize(low_c[1, u], low_s[1, u], low_bf[1, u])
+            if u == 0:
+                cast_high(1, u, True)
+            h = project("l%d" % u, [low_c[i, u][:] for i in range(2)], [low_s[i, u][:] for i in range(2)])
+            y = haar("l%d" % u, h)
+            for s in range(2):
+                nc.sync.dma_start(y_low[u * HP:(u + 1) * HP, s, :], y[s:P:2, :])
+        for i in range(2):
+            cast_high(i, 1, False)
+            quantize(high_c[i], high_s[i], high_bf[i])
+        hs = [project("h%d" % s, [high_c[i][:, s * P:(s + 1) * P] for i in range(2)],
+                      [high_s[i][:, s * P:(s + 1) * P] for i in range(2)]) for s in range(2)]
+        nc.sync.dma_start(out_rows[:, 0:2, :], y_low[:])
+        nc.vector.tensor_copy(y_bf[:, :, 0:2], y_low[:].rearrange("p s c -> p c s"))
+        for s in range(2):
+            y = haar("h%d" % s, hs[s])
+            nc.sync.dma_start(out_rows[:, 2 + s, :], y[:])
+            nc.vector.tensor_copy(y_bf[:, :, 2 + s], y[:])
+
+        y_c = sb("y_c", [P, S], U32)
+        y_s = sb("y_s", [P, S], U8)
+        nc.vector.quantize_mx(out=y_c[:].bitcast(FP8X4), scales=y_s[:], in_=y_bf[:].rearrange("p c s -> p (c s)"))
+        nc.sync.dma_start(out_1[0].rearrange("p c r -> p (c r)").bitcast(I32), y_c[:].bitcast(I32))
+        for q in range(4):
+            queue = nc.scalar if q < 2 else nc.sync
+            queue.dma_start(out_2[0, 4 * q:4 * q + 4, :].bitcast(I32), y_s[32 * q:32 * q + 4, :].bitcast(I32))

@@ -28,8 +28,8 @@ def tile_picked_othhaar_none_po_kernel(tc, x_words, x_scales, w1, w2, offs, hz, 
         keep = ctx.enter_context(tc.tile_pool(name="keep", bufs=1))
         psum = ctx.enter_context(tc.psum_pool(name="psum", bufs=1))
 
-        def sb(name, shape, dtype):
-            return keep.tile(shape, dtype, name=name, align_bytes=64)
+        def sb(name, shape, dtype, tag=None):
+            return keep.tile(shape, dtype, name=name, tag=tag or name, align_bytes=64)
 
         hz_t = sb("hz_t", [P, S // 16], U16)
         offs_t = sb("offs_t", [P, S // 16], U16)
@@ -38,24 +38,25 @@ def tile_picked_othhaar_none_po_kernel(tc, x_words, x_scales, w1, w2, offs, hz, 
         nc.sync.dma_start(hz_t[:], hz)
         nc.sync.dma_start(offs_t[:], offs)
 
-        raw = {(i, u): sb("raw%d%d" % (i, u), [P, PACK, HALF], F32) for i in range(2) for u in range(2)}
+        raw = {(i, u): [] for i in range(2) for u in range(2)}
 
-        def load_weight_half(i, u):
+        def load_weight_half(i, u, j0=0, j1=PACK, tag=None):
+            piece = sb("raw%d%d%d" % (i, u, j0), [P, j1 - j0, HALF], F32, tag)
             rows = (w1, w2)[i].rearrange("(p j) c -> p j c", j=PACK)
-            nc.sync.dma_start(raw[i, u][:], rows[:, :, u * HALF:(u + 1) * HALF])
+            nc.sync.dma_start(piece[:], rows[:, j0:j1, u * HALF:(u + 1) * HALF])
+            raw[i, u].append((piece, slice(j0, j1)))
 
         table_scales = sb("table_scales", [P, T], U8)
         nc.vector.memset(table_scales[:].bitcast(I32), 0)
-        load_weight_half(0, 0)
+        load_weight_half(0, 0, 0, 2)
         rows_by_run = x_scales[0].rearrange("(r e) c -> e r c", e=2)
         for e in range(2):
             nc.sync.dma_start(table_scales[e:P:16, :].bitcast(I32), rows_by_run[e].bitcast(I32))
 
+        load_weight_half(0, 0, 2, PACK)
         table_words = sb("table_words", [P, T], U32)
         nc.sync.dma_start(table_words[:].bitcast(I32), x_words[0].rearrange("p c r -> p (c r)").bitcast(I32))
         load_weight_half(1, 0)
-        load_weight_half(0, 1)
-        load_weight_half(1, 1)
         nc.sync.dma_start(n1_t[:], n1)
         nc.sync.dma_start(n2_t[:], n2)
 
@@ -65,7 +66,7 @@ def tile_picked_othhaar_none_po_kernel(tc, x_words, x_scales, w1, w2, offs, hz, 
         x_sc = sb("x_sc", [P, 2 * S], U8)
         nc.vector.tensor_copy(x_sc[:].bitcast(I32), picked_scales[:].bitcast(I32))
         for e in range(2):
-            nc.scalar.dma_start(x_sc[2 + e:P:32, :].bitcast(I32), picked_scales[16 + e:P:32, :].bitcast(I32))
+            nc.sync.dma_start(x_sc[2 + e:P:32, :].bitcast(I32), picked_scales[16 + e:P:32, :].bitcast(I32))
 
         x_w = [sb("x_w%d" % i, [P, S], U32) for i in range(2)]
         nc.vector.tensor_copy(x_w[0][:], table_words[:].indirect(offs_t[:]))
@@ -84,74 +85,109 @@ def tile_picked_othhaar_none_po_kernel(tc, x_words, x_scales, w1, w2, offs, hz, 
             else:
                 nc.vector.tensor_copy(out, in_)
 
-        def cast_low(i, u, on_scalar):
-            src = raw[i, u][:].rearrange("p j (m s) -> p m j s", s=PACK)[:, :, :, 0:2]
-            cast(on_scalar, low_bf[i, u][:].rearrange("p (m s j) -> p m j s", s=2, j=PACK), src)
+        def cast_low(i, u, on_scalar, m0=0, m1=HP):
+            dst = low_bf[i, u][:].rearrange("p (m s j) -> p m j s", s=2, j=PACK)
+            for piece, rows in raw[i, u]:
+                src = piece[:].rearrange("p j (m s) -> p m j s", s=PACK)[:, m0:m1, :, 0:2]
+                cast(on_scalar, dst[:, m0:m1, rows, :], src)
 
         def cast_high(i, u, on_scalar):
-            src = raw[i, u][:].rearrange("p j (m s) -> p m j s", s=PACK)[:, :, :, 2:4]
             dst = high_bf[i][:].rearrange("p (s m j) -> p m j s", s=2, j=PACK)[:, u * HP:(u + 1) * HP, :, :]
-            cast(on_scalar, dst, src)
+            for piece, rows in raw[i, u]:
+                src = piece[:].rearrange("p j (m s) -> p m j s", s=PACK)[:, :, :, 2:4]
+                cast(on_scalar, dst[:, :, rows, :], src)
 
         def quantize(codes, scales, values):
             nc.vector.quantize_mx(out=codes[:].bitcast(FP8X4), scales=scales[:], in_=values[:])
 
-        def project(name, codes, scales):
+        def project(name, codes, scales, tag=None):
             acc = psum.tile([P, S], F32, name="acc" + name)
             for i in range(2):
                 nc.tensor.matmul_mx(out=acc[:], lhsT=codes[i].bitcast(FP8X4), lhsT_scale=scales[i],
                                     rhs=x_w[i][:].bitcast(FP8X4), rhs_scale=x_sc[:, i * S:(i + 1) * S],
                                     start=(i == 0), stop=(i == 1))
-            h = sb("h" + name, [P, S], F32)
+            h = sb("h" + name, [P, S], F32, tag)
             nc.vector.tensor_copy(h[:], acc[:])
             return h
 
-        def haar(name, h):
+        def fetch(name, h):
             pa = sb("pa" + name, [P, W], F32)
             pb = sb("pb" + name, [P, W], F32)
             nc.scalar.activation(pa[:], h[:].indirect(n1_t[:]), COPY)
             nc.scalar.activation(pb[:], h[:].indirect(n2_t[:]), COPY)
+            return pa, pb
+
+        def combine(name, pa, pb):
             total = sb("total" + name, [P, W], F32)
             rb = sb("rb" + name, [P, W], F32)
             nc.vector.tensor_tensor(total[:], pa[:], pb[:], ADD)
             nc.vector.tensor_tensor(rb[:], pa[:], pb[:], SUB)
-            y = sb("y" + name, [P, S], F32)
+            return total, rb
+
+        def put_sums(y, total):
             nc.scalar.activation(y[:].indirect(n1_t[:]), total[:], COPY, scale=0.75)
+
+        def put_differences(y, rb):
             nc.scalar.activation(y[:].indirect(n2_t[:]), rb[:], COPY)
-            return y
 
         out_rows = out_0.rearrange("(p s) c -> p s c", s=PACK)
         y_low = sb("y_low", [P, 2, S], F32)
         y_bf = sb("y_bf", [P, S, PACK], BF16)
+        y = [sb("y%d" % t, [P, S], F32) for t in range(4)]
 
-        for u in range(2):
-            cast_low(0, u, u == 0)
-            quantize(low_c[0, u], low_s[0, u], low_bf[0, u])
-            if u == 0:
-                cast_high(0, u, True)
-            cast_low(1, u, False)
-            quantize(low_c[1, u], low_s[1, u], low_bf[1, u])
-            if u == 0:
-                cast_high(1, u, True)
-            h = project("l%d" % u, [low_c[i, u][:] for i in range(2)], [low_s[i, u][:] for i in range(2)])
-            y = haar("l%d" % u, h)
+        def regroup(u):
             for s in range(2):
-                nc.sync.dma_start(y_low[u * HP:(u + 1) * HP, s, :], y[s:P:2, :])
+                nc.sync.dma_start(y_low[u * HP:(u + 1) * HP, s, :], y[u][s:P:2, :])
+
+        cast_low(0, 0, True)
+        quantize(low_c[0, 0], low_s[0, 0], low_bf[0, 0])
+        cast_high(0, 0, True)
+        load_weight_half(0, 1, tag="raw002")
+        load_weight_half(1, 1, tag="low_bf00")
+        cast_low(1, 0, False)
+        quantize(low_c[1, 0], low_s[1, 0], low_bf[1, 0])
+        cast_high(1, 0, True)
+        cast_low(0, 1, True, 0, 40)
+        cast_low(0, 1, False, 40, HP)
+        cast_high(0, 1, False)
+        h0 = project("0", [low_c[i, 0][:] for i in range(2)], [low_s[i, 0][:] for i in range(2)], "raw002")
+        total0, rb0 = combine("0", *fetch("0", h0))
+        put_sums(y[0], total0)
+        put_differences(y[0], rb0)
+        regroup(0)
+
+        cast_low(1, 1, False)
+        cast_high(1, 1, False)
         for i in range(2):
-            cast_high(i, 1, False)
+            quantize(low_c[i, 1], low_s[i, 1], low_bf[i, 1])
             quantize(high_c[i], high_s[i], high_bf[i])
-        hs = [project("h%d" % s, [high_c[i][:, s * P:(s + 1) * P] for i in range(2)],
-                      [high_s[i][:, s * P:(s + 1) * P] for i in range(2)]) for s in range(2)]
+        h = {1: project("1", [low_c[i, 1][:] for i in range(2)], [low_s[i, 1][:] for i in range(2)])}
+        for s in range(2):
+            h[2 + s] = project(str(2 + s), [high_c[i][:, s * P:(s + 1) * P] for i in range(2)],
+                               [high_s[i][:, s * P:(s + 1) * P] for i in range(2)])
+        pairs = {t: fetch(str(t), h[t]) for t in (1, 2, 3)}
+        both = {t: combine(str(t), *pairs[t]) for t in (1, 2, 3)}
+        put_sums(y[1], both[1][0])
+        put_sums(y[2], both[2][0])
+        put_differences(y[1], both[1][1])
+        regroup(1)
+        put_sums(y[3], both[3][0])
+        put_differences(y[2], both[2][1])
+        put_differences(y[3], both[3][1])
+        nc.sync.dma_start(out_rows[:, 2, :], y[2][:])
+        nc.vector.tensor_copy(y_bf[:, :, 2], y[2][:])
         nc.sync.dma_start(out_rows[:, 0:2, :], y_low[:])
         nc.vector.tensor_copy(y_bf[:, :, 0:2], y_low[:].rearrange("p s c -> p c s"))
-        for s in range(2):
-            y = haar("h%d" % s, hs[s])
-            nc.sync.dma_start(out_rows[:, 2 + s, :], y[:])
-            nc.vector.tensor_copy(y_bf[:, :, 2 + s], y[:])
+        nc.sync.dma_start(out_rows[:, 3, :], y[3][:])
+        for c in range(2):
+            nc.vector.tensor_copy(y_bf[:, c * W:(c + 1) * W, 3], y[3][:, c * W:(c + 1) * W])
 
         y_c = sb("y_c", [P, S], U32)
         y_s = sb("y_s", [P, S], U8)
-        nc.vector.quantize_mx(out=y_c[:].bitcast(FP8X4), scales=y_s[:], in_=y_bf[:].rearrange("p c s -> p (c s)"))
+        for c in range(2):
+            cols = slice(c * W, (c + 1) * W)
+            nc.vector.quantize_mx(out=y_c[:, cols].bitcast(FP8X4), scales=y_s[:, cols],
+                                  in_=y_bf[:, cols, :].rearrange("p c s -> p (c s)"))
         nc.sync.dma_start(out_1[0].rearrange("p c r -> p (c r)").bitcast(I32), y_c[:].bitcast(I32))
         for q in range(4):
             queue = nc.scalar if q < 2 else nc.sync

from contextlib import ExitStack

import concourse.mybir as mybir

K, T, S, N, W = 512, 2048, 256, 512, 128
FLOPS = 2 * 2 * K * N * S

F32 = mybir.dt.float32
BF16 = mybir.dt.bfloat16
I32 = mybir.dt.int32
U32 = mybir.dt.uint32
U16 = mybir.dt.uint16
U8 = mybir.dt.uint8
FP8X4 = mybir.dt.float8_e4m3fn_x4
COPY = mybir.ActivationFunctionType.Copy
ADD = mybir.AluOpType.add
SUB = mybir.AluOpType.subtract

P = 128
PACK = 4
HALF = N // 2
HP = P // 2


def tile_picked_othhaar_none_po_kernel(tc, x_words, x_scales, w1, w2, offs, hz, n1, n2, out_0, out_1, out_2):
    nc = tc.nc
    with ExitStack() as ctx:
        keep = ctx.enter_context(tc.tile_pool(name="keep", bufs=1))
        psum = ctx.enter_context(tc.psum_pool(name="psum", bufs=1))

        def sb(name, shape, dtype, tag=None):
            return keep.tile(shape, dtype, name=name, tag=tag or name, align_bytes=64)

        hz_t = sb("hz_t", [P, S // 16], U16)
        offs_t = sb("offs_t", [P, S // 16], U16)
        n1_t = sb("n1_t", [P, W // 16], U16)
        n2_t = sb("n2_t", [P, W // 16], U16)
        nc.sync.dma_start(hz_t[:], hz)
        nc.sync.dma_start(offs_t[:], offs)

        raw = {(i, u): [] for i in range(2) for u in range(2)}

        def load_weight_half(i, u, j0=0, j1=PACK, tag=None):
            piece = sb("raw%d%d%d" % (i, u, j0), [P, j1 - j0, HALF], F32, tag)
            rows = (w1, w2)[i].rearrange("(p j) c -> p j c", j=PACK)
            nc.sync.dma_start(piece[:], rows[:, j0:j1, u * HALF:(u + 1) * HALF])
            raw[i, u].append((piece, slice(j0, j1)))

        table_scales = sb("table_scales", [P, T], U8)
        nc.vector.memset(table_scales[:].bitcast(I32), 0)
        load_weight_half(0, 0, 0, 2)
        rows_by_run = x_scales[0].rearrange("(r e) c -> e r c", e=2)
        for e in range(2):
            nc.sync.dma_start(table_scales[e:P:16, :].bitcast(I32), rows_by_run[e].bitcast(I32))

        load_weight_half(0, 0, 2, PACK)
        table_words = sb("table_words", [P, T], U32)
        nc.sync.dma_start(table_words[:].bitcast(I32), x_words[0].rearrange("p c r -> p (c r)").bitcast(I32))
        load_weight_half(1, 0)
        nc.sync.dma_start(n1_t[:], n1)
        nc.sync.dma_start(n2_t[:], n2)

        picked_scales = sb("picked_scales", [P, 2 * S], U8)
        nc.vector.tensor_copy(picked_scales[:, S:2 * S], table_scales[:].indirect(hz_t[:]))
        nc.vector.tensor_copy(picked_scales[:, 0:S], table_scales[:].indirect(offs_t[:]))
        x_sc = sb("x_sc", [P, 2 * S], U8)
        nc.vector.tensor_copy(x_sc[:].bitcast(I32), picked_scales[:].bitcast(I32))
        for e in range(2):
            nc.sync.dma_start(x_sc[2 + e:P:32, :].bitcast(I32), picked_scales[16 + e:P:32, :].bitcast(I32))

        x_w = [sb("x_w%d" % i, [P, S], U32) for i in range(2)]
        nc.vector.tensor_copy(x_w[0][:], table_words[:].indirect(offs_t[:]))
        nc.vector.tensor_copy(x_w[1][:], table_words[:].indirect(hz_t[:]))

        low_bf = {(i, u): sb("low_bf%d%d" % (i, u), [P, P * PACK], BF16) for i in range(2) for u in range(2)}
        low_c = {(i, u): sb("low_c%d%d" % (i, u), [P, P], U32) for i in range(2) for u in range(2)}
        low_s = {(i, u): sb("low_s%d%d" % (i, u), [P, P], U8) for i in range(2) for u in range(2)}
        high_bf = [sb("high_bf%d" % i, [P, 2 * P * PACK], BF16) for i in range(2)]
        high_c = [sb("high_c%d" % i, [P, 2 * P], U32) for i in range(2)]
        high_s = [sb("high_s%d" % i, [P, 2 * P], U8) for i in range(2)]

        def cast(on_scalar, out, in_):
            if on_scalar:
                nc.scalar.copy(out, in_)
            else:
                nc.vector.tensor_copy(out, in_)

        def cast_low(i, u, on_scalar, m0=0, m1=HP):
            dst = low_bf[i, u][:].rearrange("p (m s j) -> p m j s", s=2, j=PACK)
            for piece, rows in raw[i, u]:
                src = piece[:].rearrange("p j (m s) -> p m j s", s=PACK)[:, m0:m1, :, 0:2]
                cast(on_scalar, dst[:, m0:m1, rows, :], src)

        def cast_high(i, u, on_scalar):
            dst = high_bf[i][:].rearrange("p (s m j) -> p m j s", s=2, j=PACK)[:, u * HP:(u + 1) * HP, :, :]
            for piece, rows in raw[i, u]:
                src = piece[:].rearrange("p j (m s) -> p m j s", s=PACK)[:, :, :, 2:4]
                cast(on_scalar, dst[:, :, rows, :], src)

        def quantize(codes, scales, values):
            nc.vector.quantize_mx(out=codes[:].bitcast(FP8X4), scales=scales[:], in_=values[:])

        def project(name, codes, scales, tag=None):
            acc = psum.tile([P, S], F32, name="acc" + name)
            for i in range(2):
                nc.tensor.matmul_mx(out=acc[:], lhsT=codes[i].bitcast(FP8X4), lhsT_scale=scales[i],
                                    rhs=x_w[i][:].bitcast(FP8X4), rhs_scale=x_sc[:, i * S:(i + 1) * S],
                                    start=(i == 0), stop=(i == 1))
            h = sb("h" + name, [P, S], F32, tag)
            nc.vector.tensor_copy(h[:], acc[:])
            return h

        def fetch(name, h):
            pa = sb("pa" + name, [P, W], F32)
            pb = sb("pb" + name, [P, W], F32)
            nc.scalar.activation(pa[:], h[:].indirect(n1_t[:]), COPY)
            nc.scalar.activation(pb[:], h[:].indirect(n2_t[:]), COPY)
            return pa, pb

        def combine(name, pa, pb):
            total = sb("total" + name, [P, W], F32)
            rb = sb("rb" + name, [P, W], F32)
            nc.vector.tensor_tensor(total[:], pa[:], pb[:], ADD)
            nc.vector.tensor_tensor(rb[:], pa[:], pb[:], SUB)
            return total, rb

        def put_sums(y, total):
            nc.scalar.activation(y[:].indirect(n1_t[:]), total[:], COPY, scale=0.75)

        def put_differences(y, rb):
            nc.scalar.activation(y[:].indirect(n2_t[:]), rb[:], COPY)

        out_rows = out_0.rearrange("(p s) c -> p s c", s=PACK)
        y_low = sb("y_low", [P, 2, S], F32)
        y_bf = sb("y_bf", [P, S, PACK], BF16)
        y = [sb("y%d" % t, [P, S], F32) for t in range(4)]

        def regroup(u):
            for s in range(2):
                nc.sync.dma_start(y_low[u * HP:(u + 1) * HP, s, :], y[u][s:P:2, :])

        cast_low(0, 0, True)
        quantize(low_c[0, 0], low_s[0, 0], low_bf[0, 0])
        cast_high(0, 0, True)
        load_weight_half(0, 1, tag="raw002")
        load_weight_half(1, 1, tag="low_bf00")
        cast_low(1, 0, False)
        quantize(low_c[1, 0], low_s[1, 0], low_bf[1, 0])
        cast_high(1, 0, True)
        cast_low(0, 1, True, 0, 40)
        cast_low(0, 1, False, 40, HP)
        cast_high(0, 1, False)
        h0 = project("0", [low_c[i, 0][:] for i in range(2)], [low_s[i, 0][:] for i in range(2)], "raw002")
        total0, rb0 = combine("0", *fetch("0", h0))
        put_sums(y[0], total0)
        put_differences(y[0], rb0)
        regroup(0)

        cast_low(1, 1, False)
        cast_high(1, 1, False)
        for i in range(2):
            quantize(low_c[i, 1], low_s[i, 1], low_bf[i, 1])
            quantize(high_c[i], high_s[i], high_bf[i])
        h = {1: project("1", [low_c[i, 1][:] for i in range(2)], [low_s[i, 1][:] for i in range(2)])}
        for s in range(2):
            h[2 + s] = project(str(2 + s), [high_c[i][:, s * P:(s + 1) * P] for i in range(2)],
                               [high_s[i][:, s * P:(s + 1) * P] for i in range(2)])
        pairs = {t: fetch(str(t), h[t]) for t in (1, 2, 3)}
        both = {t: combine(str(t), *pairs[t]) for t in (1, 2, 3)}
        put_sums(y[1], both[1][0])
        put_sums(y[2], both[2][0])
        put_differences(y[1], both[1][1])
        regroup(1)
        put_sums(y[3], both[3][0])
        put_differences(y[2], both[2][1])
        put_differences(y[3], both[3][1])
        nc.sync.dma_start(out_rows[:, 2, :], y[2][:])
        nc.vector.tensor_copy(y_bf[:, :, 2], y[2][:])
        nc.sync.dma_start(out_rows[:, 0:2, :], y_low[:])
        nc.vector.tensor_copy(y_bf[:, :, 0:2], y_low[:].rearrange("p s c -> p c s"))
        nc.sync.dma_start(out_rows[:, 3, :], y[3][:])
        for c in range(2):
            nc.vector.tensor_copy(y_bf[:, c * W:(c + 1) * W, 3], y[3][:, c * W:(c + 1) * W])

        y_c = sb("y_c", [P, S], U32)
        y_s = sb("y_s", [P, S], U8)
        for c in range(2):
            cols = slice(c * W, (c + 1) * W)
            nc.vector.quantize_mx(out=y_c[:, cols].bitcast(FP8X4), scales=y_s[:, cols],
                                  in_=y_bf[:, cols, :].rearrange("p c s -> p (c s)"))
        nc.sync.dma_start(out_1[0].rearrange("p c r -> p (c r)").bitcast(I32), y_c[:].bitcast(I32))
        for q in range(4):
            queue = nc.scalar if q < 2 else nc.sync
            queue.dma_start(out_2[0, 4 * q:4 * q + 4, :].bitcast(I32), y_s[32 * q:32 * q + 4, :].bitcast(I32))
